import numpy as np
import ml_dtypes


def mxq(x, axis, fmt="e4m3"):
    dtype, down = {"e4m3": (ml_dtypes.float8_e4m3fn, 7), "e5m2": (ml_dtypes.float8_e5m2, 14)}[fmt]
    v = np.moveaxis(np.asarray(x, np.float32).astype(ml_dtypes.bfloat16).astype(np.float64), axis, -1)
    blocks = v.reshape(v.shape[:-1] + (-1, 32))
    amax = np.abs(blocks).max(-1, keepdims=True)
    byte = np.maximum(np.where(amax > 0, np.frexp(amax)[1] - 1 + 127, 0) - down, 1)
    scale = np.exp2(byte - 127.0)
    codes = (blocks / scale).astype(np.float32).astype(dtype).astype(np.float64)
    return np.moveaxis((codes * scale).reshape(v.shape), -1, axis)


WIDE = False


def mx_kscale(k):
    if not WIDE:
        return np.ones(k)
    levels = np.array([10, -10, 5, -5, 0])
    if k % 512:
        return np.exp2(np.random.permutation(np.resize(levels, k // 32))).repeat(32)
    a = np.empty((k // 512, 16))
    for p in range(k // 512):
        a[p, :8] = np.random.permutation(np.resize(levels, 8))
        for g in range(8):
            far = levels[np.abs(levels - a[p, g]) >= 10]
            a[p, g + 8] = far[np.random.randint(len(far))]
    return np.exp2(a.ravel()).repeat(32)


def f64(x):
    return np.asarray(x).astype(np.float64)


def striped(idx):
    return np.tile(idx.reshape(-1, 16).T, (8, 1)).astype(np.uint16)


def unstriped(offs):
    return offs[:16].T.reshape(-1).astype(np.int64)


def silu(v):
    return v / (1.0 + np.exp(-np.maximum(v, -700.0)))


K, T, E, C, H, N = 1024, 512, 8, 256, 512, 128
TOP = 4


def by_expert(wq, xq):
    return np.concatenate([wq[e].T @ xq[:, e * C:(e + 1) * C] for e in range(E)], axis=1)


def setup_inputs():
    n = np.random.standard_normal
    s = mx_kscale(K)[:, None]
    u = mx_kscale(H)
    deal = np.repeat(np.arange(E), C).reshape(TOP, T)[:, np.random.permutation(T)]
    deal = np.take_along_axis(deal, np.argsort(np.random.rand(TOP, T), axis=0), axis=0)
    for _ in range(8):
        s_, t_ = np.random.permutation(T).reshape(2, -1); r = np.random.randint(TOP, size=T // 2); x, y = deal[r, s_].copy(), deal[r, t_].copy()
        ok = ~((deal[:, s_] == y).any(0) | (deal[:, t_] == x).any(0)); deal[r[ok], s_[ok]] = y[ok]; deal[r[ok], t_[ok]] = x[ok]
    order = np.lexsort((np.random.rand(TOP * T), deal.reshape(-1)))
    slot_token = order % T; pos = np.empty(TOP * T, np.int64); pos[order] = np.arange(TOP * T); pos = pos.reshape(TOP, T)
    g = np.random.uniform(0.5, 1.5, (TOP, T)); g = g / g.sum(0)
    w_slot = np.empty(E * C)
    for r in range(TOP): w_slot[pos[r]] = g[r]
    return {
        "xT": (n((K, T)) * s).astype(np.float32),
        "w1": (n((E, K, H)) / np.sqrt(K) / s[None] * u[None, None, :]).astype(np.float32),
        "w2": (n((E, H, N)) / np.sqrt(H) / u[None, :, None]).astype(np.float32),
        "gate": np.tile(w_slot, (K, 1)).astype(np.float32),
        "offs": striped(slot_token),
        "pos1": striped(pos[0]),
        "pos2": striped(pos[1]),
        "pos3": striped(pos[2]),
        "pos4": striped(pos[3]),
    }


def reference(xT, w1, w2, gate, offs, pos1, pos2, pos3, pos4):
    idx = unstriped(offs)
    xq = mxq(f64(gate) * f64(xT)[:, idx], 0, "e4m3")
    h = silu(by_expert(mxq(f64(w1), 1, "e4m3"), xq))
    y = by_expert(mxq(f64(w2), 1, "e4m3"), mxq(h, 0, "e4m3"))
    return y[:, unstriped(pos1)] + y[:, unstriped(pos2)] + y[:, unstriped(pos3)] + y[:, unstriped(pos4)]

@@ -1,0 +1,400 @@
+from contextlib import ExitStack
+
+import concourse.mybir as mybir
+
+K, T, E, C, H, N = 1024, 512, 8, 256, 512, 128
+TOP = 4
+SLOTS = E * C
+
+FLOPS = 2 * SLOTS * (K * H + H * N)
+BYTES = 4 * (K * T + E * K * H + E * H * N + SLOTS + N * T) + 2 * 128 * (SLOTS + TOP * T) // 16
+
+F32 = mybir.dt.float32
+BF16 = mybir.dt.bfloat16
+U32 = mybir.dt.uint32
+U16 = mybir.dt.uint16
+U8 = mybir.dt.uint8
+FP8X4 = mybir.dt.float8_e4m3fn_x4
+MULT = mybir.AluOpType.mult
+ADD = mybir.AluOpType.add
+SILU = mybir.ActivationFunctionType.Silu
+
+P = 128
+PACK = 4
+K_PASS = P * PACK
+PASSES = K // K_PASS
+CHUNK = 512
+CHUNKS = SLOTS // CHUNK
+PER_CHUNK = CHUNK // C
+PAD = 16
+HALF = 128
+W2_GROUP = 4
+
+SWAPPED = (
+    ('XC',3,1,),
+    ('WC',3,0,),
+    ('WC',7,1,),
+    ('WC',5,1,),
+)
+LOADS = (
+    ('offs',),
+    ('win',0,0,),
+    ('gate',0,),
+    ('win',0,1,),
+    ('w1h',0,0,0,),
+    ('win',0,2,),
+    ('win',0,3,),
+    ('w1h',0,0,1,),
+    ('win',1,0,),
+    ('win',1,1,),
+    ('w1h',0,1,0,),
+    ('win',1,2,),
+    ('win',1,3,),
+    ('w1h',0,1,1,),
+    ('w1',1,0,),
+    ('gate',1,),
+    ('w1',1,1,),
+    ('w1',2,0,),
+    ('w1',2,1,),
+    ('w1',3,0,),
+    ('gate',2,),
+    ('w1',3,1,),
+    ('w1',4,0,),
+    ('w1',4,1,),
+    ('w1',5,0,),
+    ('gate',3,),
+    ('w1',5,1,),
+    ('w1',6,0,),
+    ('w1',6,1,),
+    ('w1',7,0,),
+    ('w2',0,),
+    ('w2',1,),
+    ('w2',2,),
+    ('w2',3,),
+    ('w1',7,1,),
+    ('w2',4,),
+    ('w2',5,),
+    ('w2',6,),
+    ('w2',7,),
+    ('pos',),
+)
+STEPS = (
+    ('G',0,0,0,),
+    ('G',0,0,1,),
+    ('G',0,0,2,),
+    ('G',0,0,3,),
+    ('WC',0,0,),
+    ('WQ',0,0,),
+    ('WC',0,1,),
+    ('WQ',0,1,),
+    ('WC',1,0,),
+    ('WQ',1,0,),
+    ('XC',0,0,),
+    ('XQ',0,0,),
+    ('G',0,1,0,),
+    ('G',0,1,1,),
+    ('G',0,1,2,),
+    ('G',0,1,3,),
+    ('WC',1,1,),
+    ('WQ',1,1,),
+    ('WC',2,0,),
+    ('WQ',2,0,),
+    ('XC',0,1,),
+    ('XQ',0,1,),
+    ('G',1,0,0,),
+    ('G',1,0,1,),
+    ('G',1,0,2,),
+    ('G',1,0,3,),
+    ('WC',2,1,),
+    ('WQ',2,1,),
+    ('WC',3,0,),
+    ('WQ',3,0,),
+    ('XC',1,0,),
+    ('XQ',1,0,),
+    ('G',1,1,0,),
+    ('G',1,1,1,),
+    ('G',1,1,2,),
+    ('G',1,1,3,),
+    ('WC',3,1,),
+    ('WQ',3,1,),
+    ('L1',0,),
+    ('HQ',0,),
+    ('WC',4,0,),
+    ('WQ',4,0,),
+    ('XC',1,1,),
+    ('XQ',1,1,),
+    ('G',2,0,0,),
+    ('G',2,0,1,),
+    ('G',2,0,2,),
+    ('G',2,0,3,),
+    ('WC',4,1,),
+    ('WQ',4,1,),
+    ('L1',1,),
+    ('HQ',1,),
+    ('WC',5,0,),
+    ('WQ',5,0,),
+    ('XC',2,0,),
+    ('XQ',2,0,),
+    ('G',2,1,0,),
+    ('G',2,1,1,),
+    ('G',2,1,2,),
+    ('G',2,1,3,),
+    ('WC',5,1,),
+    ('WQ',5,1,),
+    ('L1',2,),
+    ('HQ',2,),
+    ('WC',6,0,),
+    ('WQ',6,0,),
+    ('XC',2,1,),
+    ('XQ',2,1,),
+    ('W2C',0,),
+    ('W2Q',0,),
+    ('L2',0,),
+    ('L2',1,),
+    ('L2',2,),
+    ('G',3,0,0,),
+    ('G',3,0,1,),
+    ('G',3,0,2,),
+    ('G',3,0,3,),
+    ('WC',6,1,),
+    ('WQ',6,1,),
+    ('L1',3,),
+    ('HQ',3,),
+    ('L2',3,),
+    ('WC',7,0,),
+    ('WQ',7,0,),
+    ('XC',3,0,),
+    ('XQ',3,0,),
+    ('G',3,1,0,),
+    ('G',3,1,1,),
+    ('G',3,1,2,),
+    ('G',3,1,3,),
+    ('L1',4,),
+    ('HQ',4,),
+    ('XC',3,1,),
+    ('XQ',3,1,),
+    ('WC',7,1,),
+    ('WQ',7,1,),
+    ('L1',5,),
+    ('L1',6,),
+    ('L1',7,),
+    ('W2C',1,),
+    ('W2Q',1,),
+    ('L2',4,),
+    ('HQ',5,),
+    ('L2',5,),
+    ('HQ',6,),
+    ('L2',6,),
+    ('HQ',7,),
+    ('L2',7,),
+)
+
+
+def tile_moe_pre_mlp_silu_kernel(
+    tc, xT, w1, w2, gate, offs, pos1, pos2, pos3, pos4, out
+):
+    nc = tc.nc
+
+    with ExitStack() as ctx:
+        keep = ctx.enter_context(tc.tile_pool(name="keep", bufs=1))
+        w1_stage = ctx.enter_context(tc.tile_pool(name="w1_stage", bufs=7))
+        gathered = ctx.enter_context(tc.tile_pool(name="gathered", bufs=2))
+        rounded = ctx.enter_context(tc.tile_pool(name="rounded", bufs=3))
+        codes = ctx.enter_context(tc.tile_pool(name="codes", bufs=6))
+        psum_a = ctx.enter_context(tc.psum_pool(name="psum_a", bufs=4))
+        psum_y = ctx.enter_context(tc.psum_pool(name="psum_y", bufs=2))
+
+        def cast(on_vector, dst, src):
+            if on_vector:
+                nc.vector.tensor_copy(out=dst, in_=src)
+            else:
+                nc.scalar.copy(out=dst, in_=src)
+
+        def quantize(tag, values, words, bufs):
+            q = codes.tile([P, words], U32, name=tag + "_codes", align_bytes=64, bufs=bufs)
+            s = codes.tile([P, words], U8, name=tag + "_scales", align_bytes=64, bufs=bufs)
+            nc.vector.quantize_mx(out=q[:].bitcast(FP8X4), scales=s[:], in_=values)
+            return q, s
+
+        slot_tokens = keep.tile([P, SLOTS // 16], U16, name="slot_tokens")
+        token_slots = [keep.tile([P, T // 16], U16, name="token_slots%d" % r) for r in range(TOP)]
+        windows = {}
+        for a in range(PASSES):
+            for j in range(PACK):
+                windows[a, j] = keep.tile([P, T + PAD], F32, name="window%d%d" % (a, j))
+                nc.gpsimd.memset(windows[a, j][:, T:], 0.0)
+        gates = [keep.tile([P, CHUNK], F32, name="gate%d" % c) for c in range(CHUNKS)]
+        w2_raw = [keep.tile([P, W2_GROUP, PACK, N], F32, name="w2_raw%d" % g) for g in range(E // W2_GROUP)]
+        y_slots = keep.tile([P, SLOTS], F32, name="y_slots")
+
+        zero = keep.tile([P, 1], F32, name="zero")
+        silu_bias = keep.tile([P, 1], F32, name="silu_bias")
+        nc.gpsimd.memset(zero[:], 0.0)
+        nc.scalar.activation(out=silu_bias[:], in_=zero[:], func=SILU)
+
+        x_rows = xT.rearrange("(a p j) t -> a j p t", a=PASSES, j=PACK)
+        w1_rows = w1.rearrange("e (a p j) i -> e a p j i", a=PASSES, j=PACK)
+        w2_rows = w2.rearrange("e (m t r) n -> e r m t n", t=PACK, r=2)
+        w1_raw = {}
+
+        def load_window(a, j):
+            nc.scalar.dma_start(out=windows[a, j][:, :T], in_=x_rows[a, j])
+
+        def load_gate(c):
+            nc.sync.dma_start(out=gates[c][:], in_=gate[0:P, c * CHUNK : (c + 1) * CHUNK])
+
+        def load_w1(e, a, part, parts):
+            width = H // parts
+            raw = w1_stage.tile([P, PACK, width], F32, name="w1_raw")
+            nc.sync.dma_start(out=raw[:], in_=w1_rows[e, a][:, :, part * width : (part + 1) * width])
+            w1_raw[e, a, part] = raw
+
+        def load_w2(e):
+            for r in range(2):
+                nc.sync.dma_start(out=w2_raw[e // W2_GROUP][r:P:2, e % W2_GROUP, :, :], in_=w2_rows[e, r])
+
+        for load in LOADS:
+            if load[0] == "offs":
+                nc.sync.dma_start(slot_tokens[:], offs)
+            elif load[0] == "win":
+                load_window(load[1], load[2])
+            elif load[0] == "gate":
+                load_gate(load[1])
+            elif load[0] == "w1h":
+                load_w1(load[1], load[2], load[3], 2)
+            elif load[0] == "w1":
+                load_w1(load[1], load[2], 0, 1)
+            elif load[0] == "w2":
+                load_w2(load[1])
+            else:
+                for tile, src in zip(token_slots, (pos1, pos2, pos3, pos4)):
+                    nc.sync.dma_start(tile[:], src)
+
+        x_gathered = {}
+        x_rounded = {}
+        x_q = {}
+        w1_rounded = {}
+        w1_q = {}
+        w2_rounded = {}
+        w2_q = {}
+        h_rounded = {}
+        h_q = {}
+
+        def gather_x(c, a, j):
+            if j == 0:
+                x_gathered[c, a] = gathered.tile([P, PACK, CHUNK], F32, name="x_gathered")
+            cols = slice(c * CHUNK // 16, (c + 1) * CHUNK // 16)
+            nc.vector.tensor_tensor(
+                x_gathered[c, a][:, j, :], windows[a, j][:].indirect(slot_tokens[:, cols]), gates[c][:], MULT
+            )
+
+        def round_x(c, a):
+            b = rounded.tile([P, CHUNK * PACK], BF16, name="x_rounded", align_bytes=64, bufs=3)
+            cast(
+                ('XC', c, a) in SWAPPED,
+                b[:].rearrange("p (s r j) -> p s j r", r=4, j=PACK),
+                x_gathered[c, a][:].rearrange("p j (s r) -> p s j r", r=4),
+            )
+            x_rounded[c, a] = b
+
+        def quantize_x(c, a):
+            x_q[c, a] = quantize("x", x_rounded[c, a][:], CHUNK, 4)
+
+        def round_w1(e, a):
+            b = rounded.tile([P, H * PACK], BF16, name="w1_rounded", align_bytes=64, bufs=5)
+            parts = 2 if e == 0 else 1
+            pairs = P // 2 // parts
+            dst = b[:].rearrange("p (t m r j) -> p m t j r", t=PACK, r=2, j=PACK)
+            for part in range(parts):
+                cast(
+                    ('WC', e, a) in SWAPPED,
+                    dst[:, part * pairs : (part + 1) * pairs],
+                    w1_raw[e, a, part][:].rearrange("p j (m t r) -> p m t j r", t=PACK, r=2),
+                )
+            w1_rounded[e, a] = b
+
+        def quantize_w1(e, a):
+            w1_q[e, a] = quantize("w1", w1_rounded[e, a][:], H, 8)
+
+        def round_w2(g):
+            b = rounded.tile([P, W2_GROUP * N * PACK], BF16, name="w2_rounded", align_bytes=64, bufs=2)
+            cast(
+                ('W2C', g) not in SWAPPED,
+                b[:].rearrange("p (e s r t) -> p e s t r", e=W2_GROUP, r=4, t=PACK),
+                w2_raw[g][:].rearrange("p e t (s r) -> p e s t r", r=4),
+            )
+            w2_rounded[g] = b
+
+        def quantize_w2(g):
+            w2_q[g] = quantize("w2", w2_rounded[g][:], W2_GROUP * N, 2)
+
+        def first_layer(e):
+            c = e // PER_CHUNK
+            b = rounded.tile([P, C * PACK], BF16, name="h_rounded", align_bytes=64)
+            for half in range(C // HALF):
+                first = (e % PER_CHUNK) * C + half * HALF
+                cols = slice(first, first + HALF)
+                acc = psum_a.tile([P, PACK, HALF], F32, name="a_bank")
+                for t in range(PACK):
+                    chans = slice(t * P, (t + 1) * P)
+                    for a in range(PASSES):
+                        nc.tensor.matmul_mx(
+                            out=acc[:, t, :],
+                            lhsT=w1_q[e, a][0][:, chans].bitcast(FP8X4),
+                            lhsT_scale=w1_q[e, a][1][:, chans],
+                            rhs=x_q[c, a][0][:, cols].bitcast(FP8X4),
+                            rhs_scale=x_q[c, a][1][:, cols],
+                            start=(a == 0),
+                            stop=(a == PASSES - 1),
+                        )
+                nc.scalar.activation(
+                    out=b[:, half * HALF * PACK : (half + 1) * HALF * PACK].rearrange("p (s t) -> p s t", t=PACK),
+                    in_=acc[:].rearrange("p t s -> p s t"),
+                    func=SILU,
+                    bias=silu_bias[:],
+                )
+            h_rounded[e] = b
+
+        def quantize_h(e):
+            h_q[e] = quantize("h", h_rounded[e][:], C, 8)
+
+        def second_layer(e):
+            g = e // W2_GROUP
+            outs = slice((e % W2_GROUP) * N, (e % W2_GROUP + 1) * N)
+            acc = psum_y.tile([P, C], F32, name="y_bank")
+            nc.tensor.matmul_mx(
+                out=acc[:],
+                lhsT=w2_q[g][0][:, outs].bitcast(FP8X4),
+                lhsT_scale=w2_q[g][1][:, outs],
+                rhs=h_q[e][0][:].bitcast(FP8X4),
+                rhs_scale=h_q[e][1][:],
+                start=True,
+                stop=True,
+            )
+            nc.scalar.copy(out=y_slots[:, e * C : (e + 1) * C], in_=acc[:])
+
+        stages = {
+            "G": gather_x,
+            "XC": round_x,
+            "XQ": quantize_x,
+            "WC": round_w1,
+            "WQ": quantize_w1,
+            "L1": first_layer,
+            "HQ": quantize_h,
+            "W2C": round_w2,
+            "W2Q": quantize_w2,
+            "L2": second_layer,
+        }
+        for step in STEPS:
+            stages[step[0]](*step[1:])
+
+        picked = [keep.tile([P, T], F32, name="picked%d" % r) for r in range(TOP)]
+        sum2 = keep.tile([P, T], F32, name="sum2")
+        sum3 = keep.tile([P, T], F32, name="sum3")
+        sum4 = keep.tile([P, T], F32, name="sum4")
+        for r in range(TOP):
+            nc.vector.tensor_copy(picked[r][:], y_slots[:].indirect(token_slots[r][:]))
+        nc.vector.tensor_tensor(sum2[:], picked[0][:], picked[1][:], ADD)
+        nc.vector.tensor_tensor(sum3[:], sum2[:], picked[2][:], ADD)
+        nc.vector.tensor_tensor(sum4[:], sum3[:], picked[3][:], ADD)
+        nc.sync.dma_start(out=out, in_=sum4[:])

@@ -31,161 +31,163 @@ HALF = 128
 W2_GROUP = 4
 
 SWAPPED = (
-    ('XC',3,1,),
-    ('WC',3,0,),
-    ('WC',7,1,),
     ('WC',5,1,),
+    ('WC',7,1,),
+    ('XC',1,1,),
+    ('YC',5,),
+    ('YC',7,),
+    ('YCa',7,),
 )
 LOADS = (
     ('offs',),
-    ('win',0,0,),
     ('gate',0,),
-    ('win',0,1,),
+    ('win',0,0,),
+    ('gate',1,),
     ('w1h',0,0,0,),
-    ('win',0,2,),
-    ('win',0,3,),
+    ('win',0,1,),
     ('w1h',0,0,1,),
-    ('win',1,0,),
-    ('win',1,1,),
     ('w1h',0,1,0,),
-    ('win',1,2,),
-    ('win',1,3,),
+    ('win',0,2,),
     ('w1h',0,1,1,),
     ('w1',1,0,),
-    ('gate',1,),
+    ('win',0,3,),
+    ('win',1,0,),
+    ('win',1,1,),
+    ('win',1,2,),
     ('w1',1,1,),
+    ('win',1,3,),
     ('w1',2,0,),
     ('w1',2,1,),
     ('w1',3,0,),
-    ('gate',2,),
     ('w1',3,1,),
     ('w1',4,0,),
+    ('gate',2,),
     ('w1',4,1,),
+    ('w2',0,),
     ('w1',5,0,),
-    ('gate',3,),
     ('w1',5,1,),
+    ('gate',3,),
     ('w1',6,0,),
     ('w1',6,1,),
-    ('w1',7,0,),
-    ('w2',0,),
     ('w2',1,),
     ('w2',2,),
     ('w2',3,),
-    ('w1',7,1,),
     ('w2',4,),
     ('w2',5,),
+    ('w1',7,0,),
+    ('w1',7,1,),
     ('w2',6,),
     ('w2',7,),
     ('pos',),
 )
 STEPS = (
     ('G',0,0,0,),
-    ('G',0,0,1,),
-    ('G',0,0,2,),
-    ('G',0,0,3,),
+    ('G',1,0,0,),
     ('WC',0,0,),
-    ('WQ',0,0,),
+    ('G',0,0,1,),
+    ('G',1,0,1,),
     ('WC',0,1,),
+    ('WQ',0,0,),
+    ('G',0,0,2,),
+    ('G',1,0,2,),
     ('WQ',0,1,),
     ('WC',1,0,),
-    ('WQ',1,0,),
-    ('XC',0,0,),
-    ('XQ',0,0,),
+    ('G',0,0,3,),
+    ('G',1,0,3,),
     ('G',0,1,0,),
+    ('XC',0,0,),
     ('G',0,1,1,),
     ('G',0,1,2,),
-    ('G',0,1,3,),
-    ('WC',1,1,),
-    ('WQ',1,1,),
-    ('WC',2,0,),
-    ('WQ',2,0,),
-    ('XC',0,1,),
-    ('XQ',0,1,),
-    ('G',1,0,0,),
-    ('G',1,0,1,),
-    ('G',1,0,2,),
-    ('G',1,0,3,),
-    ('WC',2,1,),
-    ('WQ',2,1,),
-    ('WC',3,0,),
-    ('WQ',3,0,),
+    ('WQ',1,0,),
     ('XC',1,0,),
-    ('XQ',1,0,),
     ('G',1,1,0,),
     ('G',1,1,1,),
+    ('XQ',0,0,),
+    ('G',0,1,3,),
+    ('WC',1,1,),
     ('G',1,1,2,),
     ('G',1,1,3,),
-    ('WC',3,1,),
-    ('WQ',3,1,),
-    ('L1',0,),
-    ('HQ',0,),
-    ('WC',4,0,),
-    ('WQ',4,0,),
+    ('XQ',1,0,),
     ('XC',1,1,),
+    ('WC',2,0,),
+    ('WQ',1,1,),
     ('XQ',1,1,),
+    ('WC',2,1,),
+    ('WQ',2,0,),
+    ('XC',0,1,),
+    ('WQ',2,1,),
+    ('WC',3,0,),
+    ('XQ',0,1,),
+    ('WC',3,1,),
+    ('WQ',3,0,),
+    ('G',2,1,0,),
+    ('WC',4,0,),
+    ('G',2,1,1,),
     ('G',2,0,0,),
+    ('WQ',3,1,),
     ('G',2,0,1,),
+    ('L1',0,),
+    ('G',2,1,2,),
+    ('WC',4,1,),
+    ('WQ',4,0,),
     ('G',2,0,2,),
     ('G',2,0,3,),
-    ('WC',4,1,),
+    ('G',2,1,3,),
     ('WQ',4,1,),
     ('L1',1,),
-    ('HQ',1,),
+    ('HQ',0,),
     ('WC',5,0,),
     ('WQ',5,0,),
-    ('XC',2,0,),
-    ('XQ',2,0,),
-    ('G',2,1,0,),
-    ('G',2,1,1,),
-    ('G',2,1,2,),
-    ('G',2,1,3,),
-    ('WC',5,1,),
-    ('WQ',5,1,),
-    ('L1',2,),
-    ('HQ',2,),
-    ('WC',6,0,),
-    ('WQ',6,0,),
     ('XC',2,1,),
-    ('XQ',2,1,),
-    ('W2C',0,),
-    ('W2Q',0,),
-    ('L2',0,),
-    ('L2',1,),
-    ('L2',2,),
+    ('WC',5,1,),
     ('G',3,0,0,),
     ('G',3,0,1,),
-    ('G',3,0,2,),
-    ('G',3,0,3,),
-    ('WC',6,1,),
-    ('WQ',6,1,),
-    ('L1',3,),
-    ('HQ',3,),
-    ('L2',3,),
-    ('WC',7,0,),
-    ('WQ',7,0,),
-    ('XC',3,0,),
-    ('XQ',3,0,),
+    ('XC',2,0,),
     ('G',3,1,0,),
     ('G',3,1,1,),
+    ('G',3,0,2,),
     ('G',3,1,2,),
+    ('WC',6,0,),
+    ('XQ',2,1,),
     ('G',3,1,3,),
-    ('L1',4,),
-    ('HQ',4,),
+    ('XQ',2,0,),
+    ('HQ',1,),
+    ('WC',6,1,),
+    ('G',3,0,3,),
+    ('WQ',6,0,),
+    ('WQ',5,1,),
+    ('L1',2,),
+    ('WQ',6,1,),
+    ('W2C',0,),
+    ('L1',3,),
+    ('HQ',2,),
     ('XC',3,1,),
+    ('W2Q',0,),
+    ('HQ',3,),
+    ('XC',3,0,),
     ('XQ',3,1,),
+    ('WC',7,0,),
+    ('XQ',3,0,),
     ('WC',7,1,),
-    ('WQ',7,1,),
+    ('L1',4,),
+    ('WQ',7,0,),
     ('L1',5,),
-    ('L1',6,),
-    ('L1',7,),
+    ('WQ',7,1,),
+    ('HQ',4,),
     ('W2C',1,),
-    ('W2Q',1,),
-    ('L2',4,),
+    ('L2',0,),
+    ('L1',6,),
     ('HQ',5,),
-    ('L2',5,),
+    ('W2Q',1,),
+    ('L2',2,),
+    ('L2',1,),
     ('HQ',6,),
-    ('L2',6,),
+    ('L1',7,),
+    ('L2',5,),
+    ('L2',3,),
     ('HQ',7,),
+    ('L2',4,),
+    ('L2',6,),
     ('L2',7,),
 )
 
@@ -197,12 +199,12 @@ def tile_moe_pre_mlp_silu_kernel(
 
     with ExitStack() as ctx:
         keep = ctx.enter_context(tc.tile_pool(name="keep", bufs=1))
-        w1_stage = ctx.enter_context(tc.tile_pool(name="w1_stage", bufs=7))
-        gathered = ctx.enter_context(tc.tile_pool(name="gathered", bufs=2))
+        w1_stage = ctx.enter_context(tc.tile_pool(name="w1_stage", bufs=6))
+        gathered = ctx.enter_context(tc.tile_pool(name="gathered", bufs=3))
         rounded = ctx.enter_context(tc.tile_pool(name="rounded", bufs=3))
         codes = ctx.enter_context(tc.tile_pool(name="codes", bufs=6))
-        psum_a = ctx.enter_context(tc.psum_pool(name="psum_a", bufs=4))
-        psum_y = ctx.enter_context(tc.psum_pool(name="psum_y", bufs=2))
+        psum_a = ctx.enter_context(tc.psum_pool(name="psum_a", bufs=5))
+        psum_y = ctx.enter_context(tc.psum_pool(name="psum_y", bufs=3))
 
         def cast(on_vector, dst, src):
             if on_vector:
@@ -238,7 +240,8 @@ def tile_moe_pre_mlp_silu_kernel(
         w1_raw = {}
 
         def load_window(a, j):
-            nc.scalar.dma_start(out=windows[a, j][:, :T], in_=x_rows[a, j])
+            queue = nc.scalar if a * PACK + j < 0 else nc.sync
+            queue.dma_start(out=windows[a, j][:, :T], in_=x_rows[a, j])
 
         def load_gate(c):
             nc.sync.dma_start(out=gates[c][:], in_=gate[0:P, c * CHUNK : (c + 1) * CHUNK])
@@ -289,19 +292,19 @@ def tile_moe_pre_mlp_silu_kernel(
             )
 
         def round_x(c, a):
-            b = rounded.tile([P, CHUNK * PACK], BF16, name="x_rounded", align_bytes=64, bufs=3)
+            b = rounded.tile([P, CHUNK * PACK], BF16, name="x_rounded", align_bytes=64, bufs=4)
             cast(
                 ('XC', c, a) in SWAPPED,
-                b[:].rearrange("p (s r j) -> p s j r", r=4, j=PACK),
-                x_gathered[c, a][:].rearrange("p j (s r) -> p s j r", r=4),
+                b[:].rearrange("p (s r j) -> p s j r", r=2, j=PACK),
+                x_gathered[c, a][:].rearrange("p j (s r) -> p s j r", r=2),
             )
             x_rounded[c, a] = b
 
         def quantize_x(c, a):
-            x_q[c, a] = quantize("x", x_rounded[c, a][:], CHUNK, 4)
+            x_q[c, a] = quantize("x", x_rounded[c, a][:], CHUNK, 6)
 
         def round_w1(e, a):
-            b = rounded.tile([P, H * PACK], BF16, name="w1_rounded", align_bytes=64, bufs=5)
+            b = rounded.tile([P, H * PACK], BF16, name="w1_rounded", align_bytes=64, bufs=6)
             parts = 2 if e == 0 else 1
             pairs = P // 2 // parts
             dst = b[:].rearrange("p (t m r j) -> p m t j r", t=PACK, r=2, j=PACK)
@@ -320,8 +323,8 @@ def tile_moe_pre_mlp_silu_kernel(
             b = rounded.tile([P, W2_GROUP * N * PACK], BF16, name="w2_rounded", align_bytes=64, bufs=2)
             cast(
                 ('W2C', g) not in SWAPPED,
-                b[:].rearrange("p (e s r t) -> p e s t r", e=W2_GROUP, r=4, t=PACK),
-                w2_raw[g][:].rearrange("p e t (s r) -> p e s t r", r=4),
+                b[:].rearrange("p (e s r t) -> p e s t r", e=W2_GROUP, r=2, t=PACK),
+                w2_raw[g][:].rearrange("p e t (s r) -> p e s t r", r=2),
             )
             w2_rounded[g] = b
 
@@ -330,7 +333,7 @@ def tile_moe_pre_mlp_silu_kernel(
 
         def first_layer(e):
             c = e // PER_CHUNK
-            b = rounded.tile([P, C * PACK], BF16, name="h_rounded", align_bytes=64)
+            b = rounded.tile([P, C * PACK], BF16, name="h_rounded", align_bytes=64, bufs=4)
             for half in range(C // HALF):
                 first = (e % PER_CHUNK) * C + half * HALF
                 cols = slice(first, first + HALF)
@@ -355,23 +358,30 @@ def tile_moe_pre_mlp_silu_kernel(
                 )
             h_rounded[e] = b
 
+        def slot_parts(e):
+            width = HALF if e == E - 1 else C
+            return [(first, width) for first in range(0, C, width)]
+
         def quantize_h(e):
-            h_q[e] = quantize("h", h_rounded[e][:], C, 8)
+            for first, width in slot_parts(e):
+                h_q[e, first] = quantize("h", h_rounded[e][:, first * PACK : (first + width) * PACK], width, 9)
 
         def second_layer(e):
             g = e // W2_GROUP
             outs = slice((e % W2_GROUP) * N, (e % W2_GROUP + 1) * N)
-            acc = psum_y.tile([P, C], F32, name="y_bank")
-            nc.tensor.matmul_mx(
-                out=acc[:],
-                lhsT=w2_q[g][0][:, outs].bitcast(FP8X4),
-                lhsT_scale=w2_q[g][1][:, outs],
-                rhs=h_q[e][0][:].bitcast(FP8X4),
-                rhs_scale=h_q[e][1][:],
-                start=True,
-                stop=True,
-            )
-            nc.scalar.copy(out=y_slots[:, e * C : (e + 1) * C], in_=acc[:])
+            for first, width in slot_parts(e):
+                acc = psum_y.tile([P, width], F32, name="y_bank")
+                nc.tensor.matmul_mx(
+                    out=acc[:],
+                    lhsT=w2_q[g][0][:, outs].bitcast(FP8X4),
+                    lhsT_scale=w2_q[g][1][:, outs],
+                    rhs=h_q[e, first][0][:].bitcast(FP8X4),
+                    rhs_scale=h_q[e, first][1][:],
+                    start=True,
+                    stop=True,
+                )
+                kind = 'YCa' if width == HALF and first == 0 else 'YC'
+                cast((kind, e) in SWAPPED, y_slots[:, e * C + first : e * C + first + width], acc[:])
 
         stages = {
             "G": gather_x,
@@ -388,13 +398,17 @@ def tile_moe_pre_mlp_silu_kernel(
         for step in STEPS:
             stages[step[0]](*step[1:])
 
-        picked = [keep.tile([P, T], F32, name="picked%d" % r) for r in range(TOP)]
-        sum2 = keep.tile([P, T], F32, name="sum2")
-        sum3 = keep.tile([P, T], F32, name="sum3")
-        sum4 = keep.tile([P, T], F32, name="sum4")
-        for r in range(TOP):
-            nc.vector.tensor_copy(picked[r][:], y_slots[:].indirect(token_slots[r][:]))
-        nc.vector.tensor_tensor(sum2[:], picked[0][:], picked[1][:], ADD)
-        nc.vector.tensor_tensor(sum3[:], sum2[:], picked[2][:], ADD)
-        nc.vector.tensor_tensor(sum4[:], sum3[:], picked[3][:], ADD)
-        nc.sync.dma_start(out=out, in_=sum4[:])
+        picked = gathered.tile([P, TOP, T], F32, name="picked", tag="x_gathered")
+        sums = w1_stage.tile([P, TOP - 1, T], F32, name="sums", tag="w1_raw")
+
+        def pick(r):
+            nc.vector.tensor_copy(picked[:, r, :], y_slots[:].indirect(token_slots[r][:]))
+
+        pick(0)
+        pick(1)
+        pick(2)
+        nc.vector.tensor_tensor(sums[:, 0, :], picked[:, 0, :], picked[:, 1, :], ADD)
+        pick(3)
+        nc.vector.tensor_tensor(sums[:, 1, :], sums[:, 0, :], picked[:, 2, :], ADD)
+        nc.vector.tensor_tensor(sums[:, 2, :], sums[:, 1, :], picked[:, 3, :], ADD)
+        nc.sync.dma_start(out=out, in_=sums[:, 2, :])

@@ -31,50 +31,49 @@ HALF = 128
 W2_GROUP = 4
 
 SWAPPED = (
-    ('WC',5,1,),
+    ('WC',6,1,),
     ('WC',7,1,),
-    ('XC',1,1,),
-    ('YC',5,),
+    ('XC',2,1,),
+    ('YC',2,),
     ('YC',7,),
-    ('YCa',7,),
 )
 LOADS = (
     ('offs',),
-    ('gate',0,),
     ('win',0,0,),
-    ('gate',1,),
-    ('w1h',0,0,0,),
+    ('gate',0,),
     ('win',0,1,),
+    ('win',0,2,),
+    ('w1h',0,0,0,),
+    ('gate',1,),
     ('w1h',0,0,1,),
     ('w1h',0,1,0,),
-    ('win',0,2,),
     ('w1h',0,1,1,),
     ('w1',1,0,),
     ('win',0,3,),
     ('win',1,0,),
     ('win',1,1,),
-    ('win',1,2,),
     ('w1',1,1,),
+    ('win',1,2,),
     ('win',1,3,),
     ('w1',2,0,),
     ('w1',2,1,),
+    ('w2',0,),
     ('w1',3,0,),
+    ('gate',2,),
     ('w1',3,1,),
     ('w1',4,0,),
-    ('gate',2,),
     ('w1',4,1,),
-    ('w2',0,),
     ('w1',5,0,),
+    ('w2',1,),
     ('w1',5,1,),
     ('gate',3,),
     ('w1',6,0,),
     ('w1',6,1,),
-    ('w2',1,),
     ('w2',2,),
     ('w2',3,),
+    ('w1',7,0,),
     ('w2',4,),
     ('w2',5,),
-    ('w1',7,0,),
     ('w1',7,1,),
     ('w2',6,),
     ('w2',7,),
@@ -82,87 +81,87 @@ LOADS = (
 )
 STEPS = (
     ('G',0,0,0,),
-    ('G',1,0,0,),
-    ('WC',0,0,),
     ('G',0,0,1,),
-    ('G',1,0,1,),
-    ('WC',0,1,),
-    ('WQ',0,0,),
     ('G',0,0,2,),
+    ('WC',0,0,),
+    ('G',1,0,0,),
+    ('G',1,0,1,),
     ('G',1,0,2,),
+    ('WQ',0,0,),
+    ('WC',0,1,),
     ('WQ',0,1,),
     ('WC',1,0,),
     ('G',0,0,3,),
     ('G',1,0,3,),
-    ('G',0,1,0,),
+    ('G',1,1,0,),
     ('XC',0,0,),
-    ('G',0,1,1,),
-    ('G',0,1,2,),
+    ('G',1,1,1,),
     ('WQ',1,0,),
     ('XC',1,0,),
-    ('G',1,1,0,),
-    ('G',1,1,1,),
-    ('XQ',0,0,),
+    ('G',0,1,0,),
+    ('G',0,1,1,),
+    ('G',0,1,2,),
     ('G',0,1,3,),
     ('WC',1,1,),
     ('G',1,1,2,),
     ('G',1,1,3,),
+    ('XQ',0,0,),
     ('XQ',1,0,),
-    ('XC',1,1,),
     ('WC',2,0,),
     ('WQ',1,1,),
-    ('XQ',1,1,),
-    ('WC',2,1,),
-    ('WQ',2,0,),
     ('XC',0,1,),
-    ('WQ',2,1,),
-    ('WC',3,0,),
+    ('WQ',2,0,),
+    ('WC',2,1,),
     ('XQ',0,1,),
-    ('WC',3,1,),
-    ('WQ',3,0,),
+    ('WC',3,0,),
+    ('WQ',2,1,),
     ('G',2,1,0,),
-    ('WC',4,0,),
-    ('G',2,1,1,),
     ('G',2,0,0,),
-    ('WQ',3,1,),
+    ('G',2,1,1,),
+    ('XC',1,1,),
     ('G',2,0,1,),
-    ('L1',0,),
     ('G',2,1,2,),
+    ('G',2,0,2,),
+    ('G',2,1,3,),
+    ('WC',3,1,),
+    ('G',2,0,3,),
+    ('XC',2,1,),
+    ('WQ',3,0,),
+    ('WC',4,0,),
+    ('XQ',1,1,),
+    ('WQ',3,1,),
+    ('XQ',2,1,),
     ('WC',4,1,),
     ('WQ',4,0,),
-    ('G',2,0,2,),
-    ('G',2,0,3,),
-    ('G',2,1,3,),
+    ('L1',0,),
     ('WQ',4,1,),
     ('L1',1,),
     ('HQ',0,),
+    ('XC',2,0,),
+    ('HQ',1,),
+    ('G',3,1,0,),
     ('WC',5,0,),
-    ('WQ',5,0,),
-    ('XC',2,1,),
-    ('WC',5,1,),
     ('G',3,0,0,),
     ('G',3,0,1,),
-    ('XC',2,0,),
-    ('G',3,1,0,),
     ('G',3,1,1,),
     ('G',3,0,2,),
+    ('WC',5,1,),
     ('G',3,1,2,),
-    ('WC',6,0,),
-    ('XQ',2,1,),
+    ('G',3,0,3,),
     ('G',3,1,3,),
     ('XQ',2,0,),
-    ('HQ',1,),
-    ('WC',6,1,),
-    ('G',3,0,3,),
-    ('WQ',6,0,),
+    ('WC',6,0,),
     ('WQ',5,1,),
+    ('WC',6,1,),
+    ('WQ',5,0,),
     ('L1',2,),
     ('WQ',6,1,),
+    ('WQ',6,0,),
     ('W2C',0,),
     ('L1',3,),
     ('HQ',2,),
-    ('XC',3,1,),
     ('W2Q',0,),
+    ('XC',3,1,),
     ('HQ',3,),
     ('XC',3,0,),
     ('XQ',3,1,),
@@ -171,22 +170,22 @@ STEPS = (
     ('WC',7,1,),
     ('L1',4,),
     ('WQ',7,0,),
-    ('L1',5,),
     ('WQ',7,1,),
+    ('L1',5,),
     ('HQ',4,),
     ('W2C',1,),
-    ('L2',0,),
     ('L1',6,),
     ('HQ',5,),
     ('W2Q',1,),
-    ('L2',2,),
     ('L2',1,),
     ('HQ',6,),
-    ('L1',7,),
-    ('L2',5,),
     ('L2',3,),
-    ('HQ',7,),
+    ('L2',0,),
+    ('L1',7,),
+    ('L2',2,),
     ('L2',4,),
+    ('HQ',7,),
+    ('L2',5,),
     ('L2',6,),
     ('L2',7,),
 )
@@ -212,10 +211,16 @@ def tile_moe_pre_mlp_silu_kernel(
             else:
                 nc.scalar.copy(out=dst, in_=src)
 
-        def quantize(tag, values, words, bufs):
+        def quantize(tag, values, words, bufs, parts=1):
             q = codes.tile([P, words], U32, name=tag + "_codes", align_bytes=64, bufs=bufs)
             s = codes.tile([P, words], U8, name=tag + "_scales", align_bytes=64, bufs=bufs)
-            nc.vector.quantize_mx(out=q[:].bitcast(FP8X4), scales=s[:], in_=values)
+            step = words // parts
+            for first in range(0, words, step):
+                nc.vector.quantize_mx(
+                    out=q[:, first : first + step].bitcast(FP8X4),
+                    scales=s[:, first : first + step],
+                    in_=values[:, first * PACK : (first + step) * PACK],
+                )
             return q, s
 
         slot_tokens = keep.tile([P, SLOTS // 16], U16, name="slot_tokens")
@@ -292,7 +297,7 @@ def tile_moe_pre_mlp_silu_kernel(
             )
 
         def round_x(c, a):
-            b = rounded.tile([P, CHUNK * PACK], BF16, name="x_rounded", align_bytes=64, bufs=4)
+            b = rounded.tile([P, CHUNK * PACK], BF16, name="x_rounded", align_bytes=64, bufs=3)
             cast(
                 ('XC', c, a) in SWAPPED,
                 b[:].rearrange("p (s r j) -> p s j r", r=2, j=PACK),
@@ -304,7 +309,7 @@ def tile_moe_pre_mlp_silu_kernel(
             x_q[c, a] = quantize("x", x_rounded[c, a][:], CHUNK, 6)
 
         def round_w1(e, a):
-            b = rounded.tile([P, H * PACK], BF16, name="w1_rounded", align_bytes=64, bufs=6)
+            b = rounded.tile([P, H * PACK], BF16, name="w1_rounded", align_bytes=64, bufs=8)
             parts = 2 if e == 0 else 1
             pairs = P // 2 // parts
             dst = b[:].rearrange("p (t m r j) -> p m t j r", t=PACK, r=2, j=PACK)
@@ -317,7 +322,7 @@ def tile_moe_pre_mlp_silu_kernel(
             w1_rounded[e, a] = b
 
         def quantize_w1(e, a):
-            w1_q[e, a] = quantize("w1", w1_rounded[e, a][:], H, 8)
+            w1_q[e, a] = quantize("w1", w1_rounded[e, a][:], H, 6)
 
         def round_w2(g):
             b = rounded.tile([P, W2_GROUP * N * PACK], BF16, name="w2_rounded", align_bytes=64, bufs=2)
@@ -333,16 +338,17 @@ def tile_moe_pre_mlp_silu_kernel(
 
         def first_layer(e):
             c = e // PER_CHUNK
-            b = rounded.tile([P, C * PACK], BF16, name="h_rounded", align_bytes=64, bufs=4)
-            for half in range(C // HALF):
+            b = rounded.tile([P, C * PACK], BF16, name="h_rounded", align_bytes=64, bufs=5)
+            banks = [psum_a.tile([P, PACK, HALF], F32, name="a_bank") for half in range(C // HALF)]
+
+            def products(half, tiles):
                 first = (e % PER_CHUNK) * C + half * HALF
                 cols = slice(first, first + HALF)
-                acc = psum_a.tile([P, PACK, HALF], F32, name="a_bank")
-                for t in range(PACK):
+                for t in tiles:
                     chans = slice(t * P, (t + 1) * P)
                     for a in range(PASSES):
                         nc.tensor.matmul_mx(
-                            out=acc[:, t, :],
+                            out=banks[half][:, t, :],
                             lhsT=w1_q[e, a][0][:, chans].bitcast(FP8X4),
                             lhsT_scale=w1_q[e, a][1][:, chans],
                             rhs=x_q[c, a][0][:, cols].bitcast(FP8X4),
@@ -350,11 +356,17 @@ def tile_moe_pre_mlp_silu_kernel(
                             start=(a == 0),
                             stop=(a == PASSES - 1),
                         )
+
+            early = 0
+            for half in range(C // HALF):
+                products(half, range(early))
+            for half in range(C // HALF):
+                products(half, range(early, PACK))
                 nc.scalar.activation(
                     out=b[:, half * HALF * PACK : (half + 1) * HALF * PACK].rearrange("p (s t) -> p s t", t=PACK),
-                    in_=acc[:].rearrange("p t s -> p s t"),
+                    in_=banks[half][:].rearrange("p t s -> p s t"),
                     func=SILU,
-                    bias=silu_bias[:],
+                    bias=silu_bias[:] if (e, half) == (0, 0) else 0.0,
                 )
             h_rounded[e] = b
 
@@ -409,6 +421,9 @@ def tile_moe_pre_mlp_silu_kernel(
         pick(2)
         nc.vector.tensor_tensor(sums[:, 0, :], picked[:, 0, :], picked[:, 1, :], ADD)
         pick(3)
-        nc.vector.tensor_tensor(sums[:, 1, :], sums[:, 0, :], picked[:, 2, :], ADD)
-        nc.vector.tensor_tensor(sums[:, 2, :], sums[:, 1, :], picked[:, 3, :], ADD)
-        nc.sync.dma_start(out=out, in_=sums[:, 2, :])
+        halves = [slice(first, first + T // 2) for first in range(0, T, T // 2)]
+        for cols in halves:
+            nc.vector.tensor_tensor(sums[:, 1, cols], sums[:, 0, cols], picked[:, 2, cols], ADD)
+        for cols in halves:
+            nc.vector.tensor_tensor(sums[:, 2, cols], sums[:, 1, cols], picked[:, 3, cols], ADD)
+            nc.sync.dma_start(out=out[:, cols], in_=sums[:, 2, cols])

@@ -21,174 +21,50 @@ SILU = mybir.ActivationFunctionType.Silu
 
 P = 128
 PACK = 4
-K_PASS = P * PACK
-PASSES = K // K_PASS
+PASSES = K // (P * PACK)
+PER_COLUMN = 16
 CHUNK = 512
 CHUNKS = SLOTS // CHUNK
 PER_CHUNK = CHUNK // C
 PAD = 16
 HALF = 128
+LINE = 4
+PAIR = 2
 W2_GROUP = 4
+W1_HEAD_PARTS = 2
 
-SWAPPED = (
-    ('WC',6,1,),
-    ('WC',7,1,),
-    ('XC',2,1,),
-    ('YC',2,),
-    ('YC',7,),
-)
-LOADS = (
-    ('offs',),
-    ('win',0,0,),
-    ('gate',0,),
-    ('win',0,1,),
-    ('win',0,2,),
-    ('w1h',0,0,0,),
-    ('gate',1,),
-    ('w1h',0,0,1,),
-    ('w1h',0,1,0,),
-    ('w1h',0,1,1,),
-    ('w1',1,0,),
-    ('win',0,3,),
-    ('win',1,0,),
-    ('win',1,1,),
-    ('w1',1,1,),
-    ('win',1,2,),
-    ('win',1,3,),
-    ('w1',2,0,),
-    ('w1',2,1,),
-    ('w2',0,),
-    ('w1',3,0,),
-    ('gate',2,),
-    ('w1',3,1,),
-    ('w1',4,0,),
-    ('w1',4,1,),
-    ('w1',5,0,),
-    ('w2',1,),
-    ('w1',5,1,),
-    ('gate',3,),
-    ('w1',6,0,),
-    ('w1',6,1,),
-    ('w2',2,),
-    ('w2',3,),
-    ('w1',7,0,),
-    ('w2',4,),
-    ('w2',5,),
-    ('w1',7,1,),
-    ('w2',6,),
-    ('w2',7,),
-    ('pos',),
-)
-STEPS = (
-    ('G',0,0,0,),
-    ('G',0,0,1,),
-    ('G',0,0,2,),
-    ('WC',0,0,),
-    ('G',1,0,0,),
-    ('G',1,0,1,),
-    ('G',1,0,2,),
-    ('WQ',0,0,),
-    ('WC',0,1,),
-    ('WQ',0,1,),
-    ('WC',1,0,),
-    ('G',0,0,3,),
-    ('G',1,0,3,),
-    ('G',1,1,0,),
-    ('XC',0,0,),
-    ('G',1,1,1,),
-    ('WQ',1,0,),
-    ('XC',1,0,),
-    ('G',0,1,0,),
-    ('G',0,1,1,),
-    ('G',0,1,2,),
-    ('G',0,1,3,),
-    ('WC',1,1,),
-    ('G',1,1,2,),
-    ('G',1,1,3,),
-    ('XQ',0,0,),
-    ('XQ',1,0,),
-    ('WC',2,0,),
-    ('WQ',1,1,),
-    ('XC',0,1,),
-    ('WQ',2,0,),
-    ('WC',2,1,),
-    ('XQ',0,1,),
-    ('WC',3,0,),
-    ('WQ',2,1,),
-    ('G',2,1,0,),
-    ('G',2,0,0,),
-    ('G',2,1,1,),
-    ('XC',1,1,),
-    ('G',2,0,1,),
-    ('G',2,1,2,),
-    ('G',2,0,2,),
-    ('G',2,1,3,),
-    ('WC',3,1,),
-    ('G',2,0,3,),
-    ('XC',2,1,),
-    ('WQ',3,0,),
-    ('WC',4,0,),
-    ('XQ',1,1,),
-    ('WQ',3,1,),
-    ('XQ',2,1,),
-    ('WC',4,1,),
-    ('WQ',4,0,),
-    ('L1',0,),
-    ('WQ',4,1,),
-    ('L1',1,),
-    ('HQ',0,),
-    ('XC',2,0,),
-    ('HQ',1,),
-    ('G',3,1,0,),
-    ('WC',5,0,),
-    ('G',3,0,0,),
-    ('G',3,0,1,),
-    ('G',3,1,1,),
-    ('G',3,0,2,),
-    ('WC',5,1,),
-    ('G',3,1,2,),
-    ('G',3,0,3,),
-    ('G',3,1,3,),
-    ('XQ',2,0,),
-    ('WC',6,0,),
-    ('WQ',5,1,),
-    ('WC',6,1,),
-    ('WQ',5,0,),
-    ('L1',2,),
-    ('WQ',6,1,),
-    ('WQ',6,0,),
-    ('W2C',0,),
-    ('L1',3,),
-    ('HQ',2,),
-    ('W2Q',0,),
-    ('XC',3,1,),
-    ('HQ',3,),
-    ('XC',3,0,),
-    ('XQ',3,1,),
-    ('WC',7,0,),
-    ('XQ',3,0,),
-    ('WC',7,1,),
-    ('L1',4,),
-    ('WQ',7,0,),
-    ('WQ',7,1,),
-    ('L1',5,),
-    ('HQ',4,),
-    ('W2C',1,),
-    ('L1',6,),
-    ('HQ',5,),
-    ('W2Q',1,),
-    ('L2',1,),
-    ('HQ',6,),
-    ('L2',3,),
-    ('L2',0,),
-    ('L1',7,),
-    ('L2',2,),
-    ('L2',4,),
-    ('HQ',7,),
-    ('L2',5,),
-    ('L2',6,),
-    ('L2',7,),
-)
+X_ROUNDED_ON_VECTOR = ((1, 0),)
+W1_ROUNDED_ON_VECTOR = ((5, 1), (6, 1), (7, 1))
+Y_COPIED_ON_VECTOR = (1, 4, 7)
+
+W1_RAW_BUFS = 5
+GATHERED_BUFS = 3
+X_ROUNDED_BUFS = 2
+W1_ROUNDED_BUFS = 8
+H_ROUNDED_BUFS = 6
+X_CODES_BUFS = 6
+W1_CODES_BUFS = 10
+H_CODES_BUFS = E + 1
+W2_BUFS = E // W2_GROUP
+A_BANKS = 5
+Y_BANKS = 3
+
+LOADS = """
+    of xw.00 ga.0 xw.01 xw.02 h1.000 xw.03 ga.1 h1.001 xw.10 xw.11 h1.010 h1.011 w1.10
+    w1.11 w1.20 w1.21 xw.12 w1.30 xw.13 w2.0 ga.2 w1.31 w1.40 w1.41 w2.1 w1.50 ga.3
+    w1.51 w1.60 w2.2 w2.3 w1.61 w1.70 w1.71 w2.4 w2.5 w2.6 w2.7 po
+"""
+
+STEPS = """
+    gx.000 gx.001 gx.002 r1.00 gx.003 rx.00 gx.100 gx.101 gx.102 gx.103 gx.110 gx.010 gx.011 q1.00
+    r1.01 gx.111 rx.10 qx.00 q1.01 qx.10 r1.10 q1.10 r1.11 q1.11 r1.20 q1.20 r1.21 gx.012
+    gx.112 q1.21 r1.30 gx.013 gx.113 rx.01 q1.30 gx.210 gx.211 gx.212 rx.11 gx.200 gx.201 gx.213
+    gx.202 r1.31 qx.01 gx.203 qx.11 r1.40 q1.31 r1.41 q1.40 rx.21 q1.41 gx.300 r1.50 gx.301
+    gx.302 gx.303 qx.21 rx.20 q1.50 r1.51 m1.0 gx.310 qx.20 gx.311 r1.60 qh.0 q1.51 gx.312
+    gx.313 m1.1 r2.0 m1.2 q1.60 q2.0 rx.30 r1.61 qh.1 qh.2 q1.61 rx.31 qx.30 m2.1
+    m1.3 qx.31 r1.71 r1.70 qh.3 q1.71 m1.4 q1.70 m2.0 qh.4 m2.3 m1.5 r2.1 m1.6
+    q2.1 m1.7 qh.5 qh.6 m2.4 m2.2 m2.5 qh.7 m2.6 m2.7
+"""
 
 
 def tile_moe_pre_mlp_silu_kernel(
@@ -198,33 +74,38 @@ def tile_moe_pre_mlp_silu_kernel(
 
     with ExitStack() as ctx:
         keep = ctx.enter_context(tc.tile_pool(name="keep", bufs=1))
-        w1_stage = ctx.enter_context(tc.tile_pool(name="w1_stage", bufs=6))
-        gathered = ctx.enter_context(tc.tile_pool(name="gathered", bufs=3))
-        rounded = ctx.enter_context(tc.tile_pool(name="rounded", bufs=3))
-        codes = ctx.enter_context(tc.tile_pool(name="codes", bufs=6))
-        psum_a = ctx.enter_context(tc.psum_pool(name="psum_a", bufs=5))
-        psum_y = ctx.enter_context(tc.psum_pool(name="psum_y", bufs=3))
+        w1_stage = ctx.enter_context(tc.tile_pool(name="w1_stage", bufs=W1_RAW_BUFS))
+        gathered = ctx.enter_context(tc.tile_pool(name="gathered", bufs=GATHERED_BUFS))
+        rounded = ctx.enter_context(tc.tile_pool(name="rounded", bufs=1))
+        packed = ctx.enter_context(tc.tile_pool(name="packed", bufs=1))
+        psum_a = ctx.enter_context(tc.psum_pool(name="psum_a", bufs=A_BANKS))
+        psum_y = ctx.enter_context(tc.psum_pool(name="psum_y", bufs=Y_BANKS))
 
-        def cast(on_vector, dst, src):
+        def copy_on(on_vector, dst, src):
             if on_vector:
                 nc.vector.tensor_copy(out=dst, in_=src)
             else:
                 nc.scalar.copy(out=dst, in_=src)
 
-        def quantize(tag, values, words, bufs, parts=1):
-            q = codes.tile([P, words], U32, name=tag + "_codes", align_bytes=64, bufs=bufs)
-            s = codes.tile([P, words], U8, name=tag + "_scales", align_bytes=64, bufs=bufs)
-            step = words // parts
-            for first in range(0, words, step):
-                nc.vector.quantize_mx(
-                    out=q[:, first : first + step].bitcast(FP8X4),
-                    scales=s[:, first : first + step],
-                    in_=values[:, first * PACK : (first + step) * PACK],
-                )
-            return q, s
+        def quantize(tag, values, words, bufs):
+            codes = packed.tile([P, words], U32, name=tag + "_codes", align_bytes=64, bufs=bufs)
+            scales = packed.tile([P, words], U8, name=tag + "_scales", align_bytes=64, bufs=bufs)
+            nc.vector.quantize_mx(out=codes[:].bitcast(FP8X4), scales=scales[:], in_=values)
+            return codes, scales
 
-        slot_tokens = keep.tile([P, SLOTS // 16], U16, name="slot_tokens")
-        token_slots = [keep.tile([P, T // 16], U16, name="token_slots%d" % r) for r in range(TOP)]
+        def multiply(acc, stationary, stationary_cols, moving, moving_cols, start, stop):
+            nc.tensor.matmul_mx(
+                out=acc,
+                lhsT=stationary[0][:, stationary_cols].bitcast(FP8X4),
+                lhsT_scale=stationary[1][:, stationary_cols],
+                rhs=moving[0][:, moving_cols].bitcast(FP8X4),
+                rhs_scale=moving[1][:, moving_cols],
+                start=start,
+                stop=stop,
+            )
+
+        slot_tokens = keep.tile([P, SLOTS // PER_COLUMN], U16, name="slot_tokens")
+        token_slots = [keep.tile([P, T // PER_COLUMN], U16, name="token_slots%d" % r) for r in range(TOP)]
         windows = {}
         for a in range(PASSES):
             for j in range(PACK):
@@ -241,42 +122,50 @@ def tile_moe_pre_mlp_silu_kernel(
 
         x_rows = xT.rearrange("(a p j) t -> a j p t", a=PASSES, j=PACK)
         w1_rows = w1.rearrange("e (a p j) i -> e a p j i", a=PASSES, j=PACK)
-        w2_rows = w2.rearrange("e (m t r) n -> e r m t n", t=PACK, r=2)
+        w2_rows = w2.rearrange("e (m t r) n -> e r m t n", t=PACK, r=PAIR)
         w1_raw = {}
 
+        def load_offs():
+            nc.sync.dma_start(slot_tokens[:], offs)
+
         def load_window(a, j):
-            queue = nc.scalar if a * PACK + j < 0 else nc.sync
+            queue = nc.scalar if (a, j) == (0, 0) else nc.sync
             queue.dma_start(out=windows[a, j][:, :T], in_=x_rows[a, j])
 
         def load_gate(c):
             nc.sync.dma_start(out=gates[c][:], in_=gate[0:P, c * CHUNK : (c + 1) * CHUNK])
 
-        def load_w1(e, a, part, parts):
+        def load_w1_columns(e, a, part, parts):
             width = H // parts
             raw = w1_stage.tile([P, PACK, width], F32, name="w1_raw")
             nc.sync.dma_start(out=raw[:], in_=w1_rows[e, a][:, :, part * width : (part + 1) * width])
             w1_raw[e, a, part] = raw
 
-        def load_w2(e):
-            for r in range(2):
-                nc.sync.dma_start(out=w2_raw[e // W2_GROUP][r:P:2, e % W2_GROUP, :, :], in_=w2_rows[e, r])
+        def load_w1_half(e, a, part):
+            load_w1_columns(e, a, part, W1_HEAD_PARTS)
 
-        for load in LOADS:
-            if load[0] == "offs":
-                nc.sync.dma_start(slot_tokens[:], offs)
-            elif load[0] == "win":
-                load_window(load[1], load[2])
-            elif load[0] == "gate":
-                load_gate(load[1])
-            elif load[0] == "w1h":
-                load_w1(load[1], load[2], load[3], 2)
-            elif load[0] == "w1":
-                load_w1(load[1], load[2], 0, 1)
-            elif load[0] == "w2":
-                load_w2(load[1])
-            else:
-                for tile, src in zip(token_slots, (pos1, pos2, pos3, pos4)):
-                    nc.sync.dma_start(tile[:], src)
+        def load_w1(e, a):
+            load_w1_columns(e, a, 0, 1)
+
+        def load_w2(e):
+            for r in range(PAIR):
+                nc.sync.dma_start(out=w2_raw[e // W2_GROUP][r:P:PAIR, e % W2_GROUP, :, :], in_=w2_rows[e, r])
+
+        def load_positions():
+            for list_tile, positions in zip(token_slots, (pos1, pos2, pos3, pos4)):
+                nc.sync.dma_start(list_tile[:], positions)
+
+        loaders = {
+            "of": load_offs,
+            "xw": load_window,
+            "ga": load_gate,
+            "h1": load_w1_half,
+            "w1": load_w1,
+            "w2": load_w2,
+            "po": load_positions,
+        }
+        for word in LOADS.split():
+            loaders[word[:2]](*[int(digit) for digit in word[3:]])
 
         x_gathered = {}
         x_rounded = {}
@@ -291,84 +180,74 @@ def tile_moe_pre_mlp_silu_kernel(
         def gather_x(c, a, j):
             if j == 0:
                 x_gathered[c, a] = gathered.tile([P, PACK, CHUNK], F32, name="x_gathered")
-            cols = slice(c * CHUNK // 16, (c + 1) * CHUNK // 16)
+            cols = slice(c * CHUNK // PER_COLUMN, (c + 1) * CHUNK // PER_COLUMN)
             nc.vector.tensor_tensor(
                 x_gathered[c, a][:, j, :], windows[a, j][:].indirect(slot_tokens[:, cols]), gates[c][:], MULT
             )
 
         def round_x(c, a):
-            b = rounded.tile([P, CHUNK * PACK], BF16, name="x_rounded", align_bytes=64, bufs=3)
-            cast(
-                ('XC', c, a) in SWAPPED,
-                b[:].rearrange("p (s r j) -> p s j r", r=2, j=PACK),
-                x_gathered[c, a][:].rearrange("p j (s r) -> p s j r", r=2),
+            values = rounded.tile([P, CHUNK * PACK], BF16, name="x_rounded", align_bytes=64, bufs=X_ROUNDED_BUFS)
+            copy_on(
+                (c, a) in X_ROUNDED_ON_VECTOR,
+                values[:].rearrange("p (s r j) -> p s j r", r=LINE, j=PACK),
+                x_gathered[c, a][:].rearrange("p j (s r) -> p s j r", r=LINE),
             )
-            x_rounded[c, a] = b
+            x_rounded[c, a] = values
 
         def quantize_x(c, a):
-            x_q[c, a] = quantize("x", x_rounded[c, a][:], CHUNK, 6)
+            x_q[c, a] = quantize("x", x_rounded[c, a][:], CHUNK, X_CODES_BUFS)
 
         def round_w1(e, a):
-            b = rounded.tile([P, H * PACK], BF16, name="w1_rounded", align_bytes=64, bufs=8)
-            parts = 2 if e == 0 else 1
-            pairs = P // 2 // parts
-            dst = b[:].rearrange("p (t m r j) -> p m t j r", t=PACK, r=2, j=PACK)
+            values = rounded.tile([P, H * PACK], BF16, name="w1_rounded", align_bytes=64, bufs=W1_ROUNDED_BUFS)
+            parts = W1_HEAD_PARTS if e == 0 else 1
+            pairs = P // PAIR // parts
+            words = values[:].rearrange("p (t m r j) -> p m t j r", t=PACK, r=PAIR, j=PACK)
             for part in range(parts):
-                cast(
-                    ('WC', e, a) in SWAPPED,
-                    dst[:, part * pairs : (part + 1) * pairs],
-                    w1_raw[e, a, part][:].rearrange("p j (m t r) -> p m t j r", t=PACK, r=2),
+                copy_on(
+                    (e, a) in W1_ROUNDED_ON_VECTOR,
+                    words[:, part * pairs : (part + 1) * pairs],
+                    w1_raw[e, a, part][:].rearrange("p j (m t r) -> p m t j r", t=PACK, r=PAIR),
                 )
-            w1_rounded[e, a] = b
+            w1_rounded[e, a] = values
 
         def quantize_w1(e, a):
-            w1_q[e, a] = quantize("w1", w1_rounded[e, a][:], H, 6)
+            w1_q[e, a] = quantize("w1", w1_rounded[e, a][:], H, W1_CODES_BUFS)
 
         def round_w2(g):
-            b = rounded.tile([P, W2_GROUP * N * PACK], BF16, name="w2_rounded", align_bytes=64, bufs=2)
-            cast(
-                ('W2C', g) not in SWAPPED,
-                b[:].rearrange("p (e s r t) -> p e s t r", e=W2_GROUP, r=2, t=PACK),
-                w2_raw[g][:].rearrange("p e t (s r) -> p e s t r", r=2),
+            values = rounded.tile([P, W2_GROUP * N * PACK], BF16, name="w2_rounded", align_bytes=64, bufs=W2_BUFS)
+            nc.vector.tensor_copy(
+                out=values[:].rearrange("p (e s r t) -> p e s t r", e=W2_GROUP, r=LINE, t=PACK),
+                in_=w2_raw[g][:].rearrange("p e t (s r) -> p e s t r", r=LINE),
             )
-            w2_rounded[g] = b
+            w2_rounded[g] = values
 
         def quantize_w2(g):
-            w2_q[g] = quantize("w2", w2_rounded[g][:], W2_GROUP * N, 2)
+            w2_q[g] = quantize("w2", w2_rounded[g][:], W2_GROUP * N, W2_BUFS)
 
         def first_layer(e):
             c = e // PER_CHUNK
-            b = rounded.tile([P, C * PACK], BF16, name="h_rounded", align_bytes=64, bufs=5)
-            banks = [psum_a.tile([P, PACK, HALF], F32, name="a_bank") for half in range(C // HALF)]
-
-            def products(half, tiles):
+            values = rounded.tile([P, C * PACK], BF16, name="h_rounded", align_bytes=64, bufs=H_ROUNDED_BUFS)
+            for half in range(C // HALF):
+                bank = psum_a.tile([P, PACK, HALF], F32, name="a_bank")
                 first = (e % PER_CHUNK) * C + half * HALF
-                cols = slice(first, first + HALF)
-                for t in tiles:
-                    chans = slice(t * P, (t + 1) * P)
+                for t in range(PACK):
                     for a in range(PASSES):
-                        nc.tensor.matmul_mx(
-                            out=banks[half][:, t, :],
-                            lhsT=w1_q[e, a][0][:, chans].bitcast(FP8X4),
-                            lhsT_scale=w1_q[e, a][1][:, chans],
-                            rhs=x_q[c, a][0][:, cols].bitcast(FP8X4),
-                            rhs_scale=x_q[c, a][1][:, cols],
-                            start=(a == 0),
-                            stop=(a == PASSES - 1),
+                        multiply(
+                            bank[:, t, :],
+                            w1_q[e, a],
+                            slice(t * P, (t + 1) * P),
+                            x_q[c, a],
+                            slice(first, first + HALF),
+                            a == 0,
+                            a == PASSES - 1,
                         )
-
-            early = 0
-            for half in range(C // HALF):
-                products(half, range(early))
-            for half in range(C // HALF):
-                products(half, range(early, PACK))
                 nc.scalar.activation(
-                    out=b[:, half * HALF * PACK : (half + 1) * HALF * PACK].rearrange("p (s t) -> p s t", t=PACK),
-                    in_=banks[half][:].rearrange("p t s -> p s t"),
+                    out=values[:, half * HALF * PACK : (half + 1) * HALF * PACK].rearrange("p (s t) -> p s t", t=PACK),
+                    in_=bank[:].rearrange("p t s -> p s t"),
                     func=SILU,
                     bias=silu_bias[:] if (e, half) == (0, 0) else 0.0,
                 )
-            h_rounded[e] = b
+            h_rounded[e] = values
 
         def slot_parts(e):
             width = HALF if e == E - 1 else C
@@ -376,39 +255,30 @@ def tile_moe_pre_mlp_silu_kernel(
 
         def quantize_h(e):
             for first, width in slot_parts(e):
-                h_q[e, first] = quantize("h", h_rounded[e][:, first * PACK : (first + width) * PACK], width, 9)
+                values = h_rounded[e][:, first * PACK : (first + width) * PACK]
+                h_q[e, first] = quantize("h", values, width, H_CODES_BUFS)
 
         def second_layer(e):
-            g = e // W2_GROUP
             outs = slice((e % W2_GROUP) * N, (e % W2_GROUP + 1) * N)
             for first, width in slot_parts(e):
-                acc = psum_y.tile([P, width], F32, name="y_bank")
-                nc.tensor.matmul_mx(
-                    out=acc[:],
-                    lhsT=w2_q[g][0][:, outs].bitcast(FP8X4),
-                    lhsT_scale=w2_q[g][1][:, outs],
-                    rhs=h_q[e, first][0][:].bitcast(FP8X4),
-                    rhs_scale=h_q[e, first][1][:],
-                    start=True,
-                    stop=True,
-                )
-                kind = 'YCa' if width == HALF and first == 0 else 'YC'
-                cast((kind, e) in SWAPPED, y_slots[:, e * C + first : e * C + first + width], acc[:])
+                bank = psum_y.tile([P, width], F32, name="y_bank")
+                multiply(bank[:], w2_q[e // W2_GROUP], outs, h_q[e, first], slice(0, width), True, True)
+                copy_on(e in Y_COPIED_ON_VECTOR, y_slots[:, e * C + first : e * C + first + width], bank[:])
 
         stages = {
-            "G": gather_x,
-            "XC": round_x,
-            "XQ": quantize_x,
-            "WC": round_w1,
-            "WQ": quantize_w1,
-            "L1": first_layer,
-            "HQ": quantize_h,
-            "W2C": round_w2,
-            "W2Q": quantize_w2,
-            "L2": second_layer,
+            "gx": gather_x,
+            "rx": round_x,
+            "qx": quantize_x,
+            "r1": round_w1,
+            "q1": quantize_w1,
+            "m1": first_layer,
+            "qh": quantize_h,
+            "r2": round_w2,
+            "q2": quantize_w2,
+            "m2": second_layer,
         }
-        for step in STEPS:
-            stages[step[0]](*step[1:])
+        for word in STEPS.split():
+            stages[word[:2]](*[int(digit) for digit in word[3:]])
 
         picked = gathered.tile([P, TOP, T], F32, name="picked", tag="x_gathered")
         sums = w1_stage.tile([P, TOP - 1, T], F32, name="sums", tag="w1_raw")
@@ -421,9 +291,9 @@ def tile_moe_pre_mlp_silu_kernel(
         pick(2)
         nc.vector.tensor_tensor(sums[:, 0, :], picked[:, 0, :], picked[:, 1, :], ADD)
         pick(3)
-        halves = [slice(first, first + T // 2) for first in range(0, T, T // 2)]
-        for cols in halves:
+        token_halves = [slice(first, first + T // 2) for first in range(0, T, T // 2)]
+        for cols in token_halves:
             nc.vector.tensor_tensor(sums[:, 1, cols], sums[:, 0, cols], picked[:, 2, cols], ADD)
-        for cols in halves:
+        for cols in token_halves:
             nc.vector.tensor_tensor(sums[:, 2, cols], sums[:, 1, cols], picked[:, 3, cols], ADD)
             nc.sync.dma_start(out=out[:, cols], in_=sums[:, 2, cols])

@@ -28,42 +28,43 @@ CHUNKS = SLOTS // CHUNK
 PER_CHUNK = CHUNK // C
 PAD = 16
 HALF = 128
-LINE = 4
+VECTOR_RUN = 4
+SCALAR_RUN = 2
 PAIR = 2
 W2_GROUP = 4
-W1_HEAD_PARTS = 2
+W1_HALVES = 2
 
-X_ROUNDED_ON_VECTOR = ((1, 0),)
-W1_ROUNDED_ON_VECTOR = ((5, 1), (6, 1), (7, 1))
-Y_COPIED_ON_VECTOR = (1, 4, 7)
+X_ROUNDED_ON_VECTOR = ((2, 1), (3, 1))
+W1_ROUNDED_ON_VECTOR = ((7, 1),)
+Y_COPIED_ON_VECTOR = (1, 3, 7)
 
 W1_RAW_BUFS = 5
 GATHERED_BUFS = 3
-X_ROUNDED_BUFS = 2
-W1_ROUNDED_BUFS = 8
+X_ROUNDED_BUFS = 4
+W1_ROUNDED_BUFS = 7
 H_ROUNDED_BUFS = 6
 X_CODES_BUFS = 6
-W1_CODES_BUFS = 10
+W1_CODES_BUFS = 8
 H_CODES_BUFS = E + 1
 W2_BUFS = E // W2_GROUP
 A_BANKS = 5
 Y_BANKS = 3
 
 LOADS = """
-    of xw.00 ga.0 xw.01 xw.02 h1.000 xw.03 ga.1 h1.001 xw.10 xw.11 h1.010 h1.011 w1.10
-    w1.11 w1.20 w1.21 xw.12 w1.30 xw.13 w2.0 ga.2 w1.31 w1.40 w1.41 w2.1 w1.50 ga.3
-    w1.51 w1.60 w2.2 w2.3 w1.61 w1.70 w1.71 w2.4 w2.5 w2.6 w2.7 po
+    of xw.00 ga.0 xw.01 xw.02 h1.000 xw.03 xw.10 ga.1 h1.001 h1.010 h1.011 ga.2 xw.11
+    w1.10 w1.11 xw.12 ga.3 w1.20 w1.21 w1.30 xw.13 w1.31 w1.40 w2.0 w1.41 w2.1 w1.50
+    w1.51 w1.60 w2.2 w2.3 w1.61 w2.4 w1.70 w2.5 w1.71 w2.6 w2.7 po
 """
 
 STEPS = """
-    gx.000 gx.001 gx.002 r1.00 gx.003 rx.00 gx.100 gx.101 gx.102 gx.103 gx.110 gx.010 gx.011 q1.00
-    r1.01 gx.111 rx.10 qx.00 q1.01 qx.10 r1.10 q1.10 r1.11 q1.11 r1.20 q1.20 r1.21 gx.012
-    gx.112 q1.21 r1.30 gx.013 gx.113 rx.01 q1.30 gx.210 gx.211 gx.212 rx.11 gx.200 gx.201 gx.213
-    gx.202 r1.31 qx.01 gx.203 qx.11 r1.40 q1.31 r1.41 q1.40 rx.21 q1.41 gx.300 r1.50 gx.301
-    gx.302 gx.303 qx.21 rx.20 q1.50 r1.51 m1.0 gx.310 qx.20 gx.311 r1.60 qh.0 q1.51 gx.312
-    gx.313 m1.1 r2.0 m1.2 q1.60 q2.0 rx.30 r1.61 qh.1 qh.2 q1.61 rx.31 qx.30 m2.1
-    m1.3 qx.31 r1.71 r1.70 qh.3 q1.71 m1.4 q1.70 m2.0 qh.4 m2.3 m1.5 r2.1 m1.6
-    q2.1 m1.7 qh.5 qh.6 m2.4 m2.2 m2.5 qh.7 m2.6 m2.7
+    gx.000 gx.100 gx.001 r1.00 gx.210 r1.01 gx.002 gx.003 gx.101 gx.010 r1.10 gx.211 gx.102 rx.00
+    q1.00 gx.103 r1.11 rx.10 qx.00 gx.110 r1.20 r1.21 gx.111 gx.112 q1.11 q1.01 r1.30 qx.10
+    gx.011 r1.31 gx.012 gx.013 gx.300 gx.212 q1.10 gx.301 rx.01 r1.40 q1.30 gx.213 gx.113 gx.200
+    q1.21 r1.41 qx.01 q1.20 gx.201 rx.11 gx.202 q1.31 m1.0 gx.203 gx.310 r2.0 gx.302 qh.0
+    qx.11 gx.311 m1.1 r1.50 gx.303 rx.20 gx.312 gx.313 rx.21 q1.50 qh.1 r1.51 r1.60 qx.20
+    r2.1 rx.31 q2.0 r1.61 q1.41 rx.30 m1.2 qx.21 q1.40 qx.31 q1.60 q1.51 q1.61 r1.70
+    m1.3 qh.2 m1.4 qh.4 q1.70 m1.5 q2.1 qh.3 r1.71 qx.30 m2.0 q1.71 m2.2 qh.5
+    m1.6 m2.3 qh.6 m1.7 m2.1 m2.4 m2.5 qh.7 m2.6 m2.7
 """
 
 
@@ -142,7 +143,7 @@ def tile_moe_pre_mlp_silu_kernel(
             w1_raw[e, a, part] = raw
 
         def load_w1_half(e, a, part):
-            load_w1_columns(e, a, part, W1_HEAD_PARTS)
+            load_w1_columns(e, a, part, W1_HALVES)
 
         def load_w1(e, a):
             load_w1_columns(e, a, 0, 1)
@@ -187,10 +188,12 @@ def tile_moe_pre_mlp_silu_kernel(
 
         def round_x(c, a):
             values = rounded.tile([P, CHUNK * PACK], BF16, name="x_rounded", align_bytes=64, bufs=X_ROUNDED_BUFS)
+            on_vector = (c, a) in X_ROUNDED_ON_VECTOR
+            run = VECTOR_RUN if on_vector else SCALAR_RUN
             copy_on(
-                (c, a) in X_ROUNDED_ON_VECTOR,
-                values[:].rearrange("p (s r j) -> p s j r", r=LINE, j=PACK),
-                x_gathered[c, a][:].rearrange("p j (s r) -> p s j r", r=LINE),
+                on_vector,
+                values[:].rearrange("p (s r j) -> p s j r", r=run, j=PACK),
+                x_gathered[c, a][:].rearrange("p j (s r) -> p s j r", r=run),
             )
             x_rounded[c, a] = values
 
@@ -199,7 +202,7 @@ def tile_moe_pre_mlp_silu_kernel(
 
         def round_w1(e, a):
             values = rounded.tile([P, H * PACK], BF16, name="w1_rounded", align_bytes=64, bufs=W1_ROUNDED_BUFS)
-            parts = W1_HEAD_PARTS if e == 0 else 1
+            parts = W1_HALVES if e == 0 else 1
             pairs = P // PAIR // parts
             words = values[:].rearrange("p (t m r j) -> p m t j r", t=PACK, r=PAIR, j=PACK)
             for part in range(parts):
@@ -216,8 +219,8 @@ def tile_moe_pre_mlp_silu_kernel(
         def round_w2(g):
             values = rounded.tile([P, W2_GROUP * N * PACK], BF16, name="w2_rounded", align_bytes=64, bufs=W2_BUFS)
             nc.vector.tensor_copy(
-                out=values[:].rearrange("p (e s r t) -> p e s t r", e=W2_GROUP, r=LINE, t=PACK),
-                in_=w2_raw[g][:].rearrange("p e t (s r) -> p e s t r", r=LINE),
+                out=values[:].rearrange("p (e s r t) -> p e s t r", e=W2_GROUP, r=VECTOR_RUN, t=PACK),
+                in_=w2_raw[g][:].rearrange("p e t (s r) -> p e s t r", r=VECTOR_RUN),
             )
             w2_rounded[g] = values
 

from contextlib import ExitStack

import concourse.mybir as mybir

K, T, E, C, H, N = 1024, 512, 8, 256, 512, 128
TOP = 4
SLOTS = E * C

FLOPS = 2 * SLOTS * (K * H + H * N)
BYTES = 4 * (K * T + E * K * H + E * H * N + SLOTS + N * T) + 2 * 128 * (SLOTS + TOP * T) // 16

F32 = mybir.dt.float32
BF16 = mybir.dt.bfloat16
U32 = mybir.dt.uint32
U16 = mybir.dt.uint16
U8 = mybir.dt.uint8
FP8X4 = mybir.dt.float8_e4m3fn_x4
MULT = mybir.AluOpType.mult
ADD = mybir.AluOpType.add
SILU = mybir.ActivationFunctionType.Silu

P = 128
PACK = 4
PASSES = K // (P * PACK)
PER_COLUMN = 16
CHUNK = 512
CHUNKS = SLOTS // CHUNK
PER_CHUNK = CHUNK // C
PAD = 16
HALF = 128
VECTOR_RUN = 4
SCALAR_RUN = 2
PAIR = 2
W2_GROUP = 4
W1_HALVES = 2

X_ROUNDED_ON_VECTOR = ((2, 1), (3, 1))
W1_ROUNDED_ON_VECTOR = ((7, 1),)
Y_COPIED_ON_VECTOR = (1, 3, 7)

W1_RAW_BUFS = 5
GATHERED_BUFS = 3
X_ROUNDED_BUFS = 4
W1_ROUNDED_BUFS = 7
H_ROUNDED_BUFS = 6
X_CODES_BUFS = 6
W1_CODES_BUFS = 8
H_CODES_BUFS = E + 1
W2_BUFS = E // W2_GROUP
A_BANKS = 5
Y_BANKS = 3

LOADS = """
    of xw.00 ga.0 xw.01 xw.02 h1.000 xw.03 xw.10 ga.1 h1.001 h1.010 h1.011 ga.2 xw.11
    w1.10 w1.11 xw.12 ga.3 w1.20 w1.21 w1.30 xw.13 w1.31 w1.40 w2.0 w1.41 w2.1 w1.50
    w1.51 w1.60 w2.2 w2.3 w1.61 w2.4 w1.70 w2.5 w1.71 w2.6 w2.7 po
"""

STEPS = """
    gx.000 gx.100 gx.001 r1.00 gx.210 r1.01 gx.002 gx.003 gx.101 gx.010 r1.10 gx.211 gx.102 rx.00
    q1.00 gx.103 r1.11 rx.10 qx.00 gx.110 r1.20 r1.21 gx.111 gx.112 q1.11 q1.01 r1.30 qx.10
    gx.011 r1.31 gx.012 gx.013 gx.300 gx.212 q1.10 gx.301 rx.01 r1.40 q1.30 gx.213 gx.113 gx.200
    q1.21 r1.41 qx.01 q1.20 gx.201 rx.11 gx.202 q1.31 m1.0 gx.203 gx.310 r2.0 gx.302 qh.0
    qx.11 gx.311 m1.1 r1.50 gx.303 rx.20 gx.312 gx.313 rx.21 q1.50 qh.1 r1.51 r1.60 qx.20
    r2.1 rx.31 q2.0 r1.61 q1.41 rx.30 m1.2 qx.21 q1.40 qx.31 q1.60 q1.51 q1.61 r1.70
    m1.3 qh.2 m1.4 qh.4 q1.70 m1.5 q2.1 qh.3 r1.71 qx.30 m2.0 q1.71 m2.2 qh.5
    m1.6 m2.3 qh.6 m1.7 m2.1 m2.4 m2.5 qh.7 m2.6 m2.7
"""


def tile_moe_pre_mlp_silu_kernel(
    tc, xT, w1, w2, gate, offs, pos1, pos2, pos3, pos4, out
):
    nc = tc.nc

    with ExitStack() as ctx:
        keep = ctx.enter_context(tc.tile_pool(name="keep", bufs=1))
        w1_stage = ctx.enter_context(tc.tile_pool(name="w1_stage", bufs=W1_RAW_BUFS))
        gathered = ctx.enter_context(tc.tile_pool(name="gathered", bufs=GATHERED_BUFS))
        rounded = ctx.enter_context(tc.tile_pool(name="rounded", bufs=1))
        packed = ctx.enter_context(tc.tile_pool(name="packed", bufs=1))
        psum_a = ctx.enter_context(tc.psum_pool(name="psum_a", bufs=A_BANKS))
        psum_y = ctx.enter_context(tc.psum_pool(name="psum_y", bufs=Y_BANKS))

        def copy_on(on_vector, dst, src):
            if on_vector:
                nc.vector.tensor_copy(out=dst, in_=src)
            else:
                nc.scalar.copy(out=dst, in_=src)

        def quantize(tag, values, words, bufs):
            codes = packed.tile([P, words], U32, name=tag + "_codes", align_bytes=64, bufs=bufs)
            scales = packed.tile([P, words], U8, name=tag + "_scales", align_bytes=64, bufs=bufs)
            nc.vector.quantize_mx(out=codes[:].bitcast(FP8X4), scales=scales[:], in_=values)
            return codes, scales

        def multiply(acc, stationary, stationary_cols, moving, moving_cols, start, stop):
            nc.tensor.matmul_mx(
                out=acc,
                lhsT=stationary[0][:, stationary_cols].bitcast(FP8X4),
                lhsT_scale=stationary[1][:, stationary_cols],
                rhs=moving[0][:, moving_cols].bitcast(FP8X4),
                rhs_scale=moving[1][:, moving_cols],
                start=start,
                stop=stop,
            )

        slot_tokens = keep.tile([P, SLOTS // PER_COLUMN], U16, name="slot_tokens")
        token_slots = [keep.tile([P, T // PER_COLUMN], U16, name="token_slots%d" % r) for r in range(TOP)]
        windows = {}
        for a in range(PASSES):
            for j in range(PACK):
                windows[a, j] = keep.tile([P, T + PAD], F32, name="window%d%d" % (a, j))
                nc.gpsimd.memset(windows[a, j][:, T:], 0.0)
        gates = [keep.tile([P, CHUNK], F32, name="gate%d" % c) for c in range(CHUNKS)]
        w2_raw = [keep.tile([P, W2_GROUP, PACK, N], F32, name="w2_raw%d" % g) for g in range(E // W2_GROUP)]
        y_slots = keep.tile([P, SLOTS], F32, name="y_slots")

        zero = keep.tile([P, 1], F32, name="zero")
        silu_bias = keep.tile([P, 1], F32, name="silu_bias")
        nc.gpsimd.memset(zero[:], 0.0)
        nc.scalar.activation(out=silu_bias[:], in_=zero[:], func=SILU)

        x_rows = xT.rearrange("(a p j) t -> a j p t", a=PASSES, j=PACK)
        w1_rows = w1.rearrange("e (a p j) i -> e a p j i", a=PASSES, j=PACK)
        w2_rows = w2.rearrange("e (m t r) n -> e r m t n", t=PACK, r=PAIR)
        w1_raw = {}

        def load_offs():
            nc.sync.dma_start(slot_tokens[:], offs)

        def load_window(a, j):
            queue = nc.scalar if (a, j) == (0, 0) else nc.sync
            queue.dma_start(out=windows[a, j][:, :T], in_=x_rows[a, j])

        def load_gate(c):
            nc.sync.dma_start(out=gates[c][:], in_=gate[0:P, c * CHUNK : (c + 1) * CHUNK])

        def load_w1_columns(e, a, part, parts):
            width = H // parts
            raw = w1_stage.tile([P, PACK, width], F32, name="w1_raw")
            nc.sync.dma_start(out=raw[:], in_=w1_rows[e, a][:, :, part * width : (part + 1) * width])
            w1_raw[e, a, part] = raw

        def load_w1_half(e, a, part):
            load_w1_columns(e, a, part, W1_HALVES)

        def load_w1(e, a):
            load_w1_columns(e, a, 0, 1)

        def load_w2(e):
            for r in range(PAIR):
                nc.sync.dma_start(out=w2_raw[e // W2_GROUP][r:P:PAIR, e % W2_GROUP, :, :], in_=w2_rows[e, r])

        def load_positions():
            for list_tile, positions in zip(token_slots, (pos1, pos2, pos3, pos4)):
                nc.sync.dma_start(list_tile[:], positions)

        loaders = {
            "of": load_offs,
            "xw": load_window,
            "ga": load_gate,
            "h1": load_w1_half,
            "w1": load_w1,
            "w2": load_w2,
            "po": load_positions,
        }
        for word in LOADS.split():
            loaders[word[:2]](*[int(digit) for digit in word[3:]])

        x_gathered = {}
        x_rounded = {}
        x_q = {}
        w1_rounded = {}
        w1_q = {}
        w2_rounded = {}
        w2_q = {}
        h_rounded = {}
        h_q = {}

        def gather_x(c, a, j):
            if j == 0:
                x_gathered[c, a] = gathered.tile([P, PACK, CHUNK], F32, name="x_gathered")
            cols = slice(c * CHUNK // PER_COLUMN, (c + 1) * CHUNK // PER_COLUMN)
            nc.vector.tensor_tensor(
                x_gathered[c, a][:, j, :], windows[a, j][:].indirect(slot_tokens[:, cols]), gates[c][:], MULT
            )

        def round_x(c, a):
            values = rounded.tile([P, CHUNK * PACK], BF16, name="x_rounded", align_bytes=64, bufs=X_ROUNDED_BUFS)
            on_vector = (c, a) in X_ROUNDED_ON_VECTOR
            run = VECTOR_RUN if on_vector else SCALAR_RUN
            copy_on(
                on_vector,
                values[:].rearrange("p (s r j) -> p s j r", r=run, j=PACK),
                x_gathered[c, a][:].rearrange("p j (s r) -> p s j r", r=run),
            )
            x_rounded[c, a] = values

        def quantize_x(c, a):
            x_q[c, a] = quantize("x", x_rounded[c, a][:], CHUNK, X_CODES_BUFS)

        def round_w1(e, a):
            values = rounded.tile([P, H * PACK], BF16, name="w1_rounded", align_bytes=64, bufs=W1_ROUNDED_BUFS)
            parts = W1_HALVES if e == 0 else 1
            pairs = P // PAIR // parts
            words = values[:].rearrange("p (t m r j) -> p m t j r", t=PACK, r=PAIR, j=PACK)
            for part in range(parts):
                copy_on(
                    (e, a) in W1_ROUNDED_ON_VECTOR,
                    words[:, part * pairs : (part + 1) * pairs],
                    w1_raw[e, a, part][:].rearrange("p j (m t r) -> p m t j r", t=PACK, r=PAIR),
                )
            w1_rounded[e, a] = values

        def quantize_w1(e, a):
            w1_q[e, a] = quantize("w1", w1_rounded[e, a][:], H, W1_CODES_BUFS)

        def round_w2(g):
            values = rounded.tile([P, W2_GROUP * N * PACK], BF16, name="w2_rounded", align_bytes=64, bufs=W2_BUFS)
            nc.vector.tensor_copy(
                out=values[:].rearrange("p (e s r t) -> p e s t r", e=W2_GROUP, r=VECTOR_RUN, t=PACK),
                in_=w2_raw[g][:].rearrange("p e t (s r) -> p e s t r", r=VECTOR_RUN),
            )
            w2_rounded[g] = values

        def quantize_w2(g):
            w2_q[g] = quantize("w2", w2_rounded[g][:], W2_GROUP * N, W2_BUFS)

        def first_layer(e):
            c = e // PER_CHUNK
            values = rounded.tile([P, C * PACK], BF16, name="h_rounded", align_bytes=64, bufs=H_ROUNDED_BUFS)
            for half in range(C // HALF):
                bank = psum_a.tile([P, PACK, HALF], F32, name="a_bank")
                first = (e % PER_CHUNK) * C + half * HALF
                for t in range(PACK):
                    for a in range(PASSES):
                        multiply(
                            bank[:, t, :],
                            w1_q[e, a],
                            slice(t * P, (t + 1) * P),
                            x_q[c, a],
                            slice(first, first + HALF),
                            a == 0,
                            a == PASSES - 1,
                        )
                nc.scalar.activation(
                    out=values[:, half * HALF * PACK : (half + 1) * HALF * PACK].rearrange("p (s t) -> p s t", t=PACK),
                    in_=bank[:].rearrange("p t s -> p s t"),
                    func=SILU,
                    bias=silu_bias[:] if (e, half) == (0, 0) else 0.0,
                )
            h_rounded[e] = values

        def slot_parts(e):
            width = HALF if e == E - 1 else C
            return [(first, width) for first in range(0, C, width)]

        def quantize_h(e):
            for first, width in slot_parts(e):
                values = h_rounded[e][:, first * PACK : (first + width) * PACK]
                h_q[e, first] = quantize("h", values, width, H_CODES_BUFS)

        def second_layer(e):
            outs = slice((e % W2_GROUP) * N, (e % W2_GROUP + 1) * N)
            for first, width in slot_parts(e):
                bank = psum_y.tile([P, width], F32, name="y_bank")
                multiply(bank[:], w2_q[e // W2_GROUP], outs, h_q[e, first], slice(0, width), True, True)
                copy_on(e in Y_COPIED_ON_VECTOR, y_slots[:, e * C + first : e * C + first + width], bank[:])

        stages = {
            "gx": gather_x,
            "rx": round_x,
            "qx": quantize_x,
            "r1": round_w1,
            "q1": quantize_w1,
            "m1": first_layer,
            "qh": quantize_h,
            "r2": round_w2,
            "q2": quantize_w2,
            "m2": second_layer,
        }
        for word in STEPS.split():
            stages[word[:2]](*[int(digit) for digit in word[3:]])

        picked = gathered.tile([P, TOP, T], F32, name="picked", tag="x_gathered")
        sums = w1_stage.tile([P, TOP - 1, T], F32, name="sums", tag="w1_raw")

        def pick(r):
            nc.vector.tensor_copy(picked[:, r, :], y_slots[:].indirect(token_slots[r][:]))

        pick(0)
        pick(1)
        pick(2)
        nc.vector.tensor_tensor(sums[:, 0, :], picked[:, 0, :], picked[:, 1, :], ADD)
        pick(3)
        token_halves = [slice(first, first + T // 2) for first in range(0, T, T // 2)]
        for cols in token_halves:
            nc.vector.tensor_tensor(sums[:, 1, cols], sums[:, 0, cols], picked[:, 2, cols], ADD)
        for cols in token_halves:
            nc.vector.tensor_tensor(sums[:, 2, cols], sums[:, 1, cols], picked[:, 3, cols], ADD)
            nc.sync.dma_start(out=out[:, cols], in_=sums[:, 2, cols])
